import numpy as np
CORES = [0,1,2,3,4,5,6,7]
N = 8
ROOT = 4
def setup_inputs(rng):
    return {"x": rng.standard_normal((N, 128, N * 256), dtype=np.float32)}
def reference(x):
    return {"y": np.stack([x[ROOT][:, r * 256:(r + 1) * 256] for r in range(N)])}

@@ -1,0 +1,42 @@
+W = 256
+
+SCRATCH = {
+    "stage": ("sbuf", [128, 8 * W], "float32"),
+    "land": ("sbuf", [128, W], "float32"),
+}
+SEMAPHORES = ["ld0", "ld1", "ld2", "ld3", "ld4", "ld5", "ld6", "ld7", "sent", "arrived", "stored"]
+
+
+def rank_program(g, core, T, topo):
+    rank = T.rank_of(core)
+    if rank is None:
+        return
+    root = 4
+    root_core = T.cores[root]
+
+    if rank != root:
+        g.sync.wait_ge(T.sem.arrived, 16)
+        g.sync.dma_start(T.y[:], T.land[:]).then_inc(T.sem.stored, 16)
+        g.sync.wait_ge(T.sem.stored, 16)
+        return
+
+    others = [r for r in range(len(T.cores)) if r != root]
+    order = ([r for r in others if topo.die(T.cores[r]) != topo.die(root_core)]
+             + [r for r in others if topo.die(T.cores[r]) == topo.die(root_core)])
+
+    queues = [g.sync, g.scalar]
+    for i, r in enumerate(order):
+        cols = slice(r * W, (r + 1) * W)
+        queues[i % 2].dma_start(T.stage[:, cols], T.x[:, cols]).then_inc(T.sem["ld%d" % r], 16)
+    own = slice(root * W, (root + 1) * W)
+    queues[len(order) % 2].dma_start(T.y[:], T.x[:, own]).then_inc(T.sem["ld%d" % root], 16)
+
+    for r in order:
+        dst = T.cores[r]
+        rid, pid, _se = topo.addr(dst)
+        cols = slice(r * W, (r + 1) * W)
+        g.wait_ge(T.sem["ld%d" % r], 16)
+        g.remote_dma(T.land[:], T.stage[:, cols], T.sem.arrived, T.sem.sent, pid, rid, topo.mask(core, dst))
+
+    g.wait_ge(T.sem.sent, 16 * len(order))
+    g.wait_ge(T.sem["ld%d" % root], 16)

@@ -1,8 +1,8 @@
 W = 256
 
 SCRATCH = {
-    "stage": ("sbuf", [128, 8 * W], "float32"),
-    "land": ("sbuf", [128, W], "float32"),
+    "stage": ("dram", [8, 128, W], "float32"),
+    "land": ("dram", [128, W], "float32"),
 }
 SEMAPHORES = ["ld0", "ld1", "ld2", "ld3", "ld4", "ld5", "ld6", "ld7", "sent", "arrived", "stored"]
 
@@ -26,17 +26,14 @@ def rank_program(g, core, T, topo):
 
     queues = [g.sync, g.scalar]
     for i, r in enumerate(order):
-        cols = slice(r * W, (r + 1) * W)
-        queues[i % 2].dma_start(T.stage[:, cols], T.x[:, cols]).then_inc(T.sem["ld%d" % r], 16)
-    own = slice(root * W, (root + 1) * W)
-    queues[len(order) % 2].dma_start(T.y[:], T.x[:, own]).then_inc(T.sem["ld%d" % root], 16)
+        queues[i % 2].dma_start(T.stage[r], T.x[:, r * W:(r + 1) * W]).then_inc(T.sem["ld%d" % r], 16)
+    queues[len(order) % 2].dma_start(T.y[:], T.x[:, root * W:(root + 1) * W]).then_inc(T.sem["ld%d" % root], 16)
 
     for r in order:
         dst = T.cores[r]
         rid, pid, _se = topo.addr(dst)
-        cols = slice(r * W, (r + 1) * W)
         g.wait_ge(T.sem["ld%d" % r], 16)
-        g.remote_dma(T.land[:], T.stage[:, cols], T.sem.arrived, T.sem.sent, pid, rid, topo.mask(core, dst))
+        g.remote_dma(T.land[:], T.stage[r], T.sem.arrived, T.sem.sent, pid, rid, topo.mask(core, dst))
 
     g.wait_ge(T.sem.sent, 16 * len(order))
     g.wait_ge(T.sem["ld%d" % root], 16)

W = 256

SCRATCH = {
    "stage": ("dram", [8, 128, W], "float32"),
    "land": ("dram", [128, W], "float32"),
}
SEMAPHORES = ["ld0", "ld1", "ld2", "ld3", "ld4", "ld5", "ld6", "ld7", "sent", "arrived", "stored"]


def rank_program(g, core, T, topo):
    rank = T.rank_of(core)
    if rank is None:
        return
    root = 4
    root_core = T.cores[root]

    if rank != root:
        g.sync.wait_ge(T.sem.arrived, 16)
        g.sync.dma_start(T.y[:], T.land[:]).then_inc(T.sem.stored, 16)
        g.sync.wait_ge(T.sem.stored, 16)
        return

    others = [r for r in range(len(T.cores)) if r != root]
    order = ([r for r in others if topo.die(T.cores[r]) != topo.die(root_core)]
             + [r for r in others if topo.die(T.cores[r]) == topo.die(root_core)])

    queues = [g.sync, g.scalar]
    for i, r in enumerate(order):
        queues[i % 2].dma_start(T.stage[r], T.x[:, r * W:(r + 1) * W]).then_inc(T.sem["ld%d" % r], 16)
    queues[len(order) % 2].dma_start(T.y[:], T.x[:, root * W:(root + 1) * W]).then_inc(T.sem["ld%d" % root], 16)

    for r in order:
        dst = T.cores[r]
        rid, pid, _se = topo.addr(dst)
        g.wait_ge(T.sem["ld%d" % r], 16)
        g.remote_dma(T.land[:], T.stage[r], T.sem.arrived, T.sem.sent, pid, rid, topo.mask(core, dst))

    g.wait_ge(T.sem.sent, 16 * len(order))
    g.wait_ge(T.sem["ld%d" % root], 16)
